import numpy as np
import ml_dtypes


def mxq(x, axis, fmt="e4m3"):
    dtype, down = {"e4m3": (ml_dtypes.float8_e4m3fn, 7), "e5m2": (ml_dtypes.float8_e5m2, 14)}[fmt]
    v = np.moveaxis(np.asarray(x, np.float32).astype(ml_dtypes.bfloat16).astype(np.float64), axis, -1)
    blocks = v.reshape(v.shape[:-1] + (-1, 32))
    amax = np.abs(blocks).max(-1, keepdims=True)
    byte = np.maximum(np.where(amax > 0, np.frexp(amax)[1] - 1 + 127, 0) - down, 1)
    scale = np.exp2(byte - 127.0)
    codes = (blocks / scale).astype(np.float32).astype(dtype).astype(np.float64)
    return np.moveaxis((codes * scale).reshape(v.shape), -1, axis)


WIDE = False


def mx_kscale(k):
    if not WIDE:
        return np.ones(k)
    levels = np.array([10, -10, 5, -5, 0])
    if k % 512:
        return np.exp2(np.random.permutation(np.resize(levels, k // 32))).repeat(32)
    a = np.empty((k // 512, 16))
    for p in range(k // 512):
        a[p, :8] = np.random.permutation(np.resize(levels, 8))
        for g in range(8):
            far = levels[np.abs(levels - a[p, g]) >= 10]
            a[p, g + 8] = far[np.random.randint(len(far))]
    return np.exp2(a.ravel()).repeat(32)


def f64(x):
    return np.asarray(x).astype(np.float64)


def striped(idx):
    return np.tile(idx.reshape(-1, 16).T, (8, 1)).astype(np.uint16)


def unstriped(offs):
    return offs[:16].T.reshape(-1).astype(np.int64)


K, T, E, C, N = 512, 768, 24, 128, 384
TOP = 4


def by_expert(wq, xq):
    return np.concatenate([wq[e].T @ xq[:, e * C:(e + 1) * C] for e in range(E)], axis=1)


def setup_inputs():
    n = np.random.standard_normal
    s = mx_kscale(K)[:, None]
    deal = np.repeat(np.arange(E), C).reshape(TOP, T)[:, np.random.permutation(T)]
    deal = np.take_along_axis(deal, np.argsort(np.random.rand(TOP, T), axis=0), axis=0)
    for _ in range(8):
        s_, t_ = np.random.permutation(T).reshape(2, -1); r = np.random.randint(TOP, size=T // 2); x, y = deal[r, s_].copy(), deal[r, t_].copy()
        ok = ~((deal[:, s_] == y).any(0) | (deal[:, t_] == x).any(0)); deal[r[ok], s_[ok]] = y[ok]; deal[r[ok], t_[ok]] = x[ok]
    order = np.lexsort((np.random.rand(TOP * T), deal.reshape(-1)))
    slot_token = order % T; pos = np.empty(TOP * T, np.int64); pos[order] = np.arange(TOP * T); pos = pos.reshape(TOP, T)
    g = np.random.uniform(0.5, 1.5, (TOP, T)); g = g / g.sum(0)
    return {
        "xT": (n((K, T)) * s).astype(np.float32),
        "w": (n((E, K, N)) / np.sqrt(K) / s[None]).astype(np.float32),
        "b": (0.3 * n((N, E))).astype(np.float32),
        "gate": np.stack([np.tile(r, (N, 1)) for r in g]).astype(np.float32),
        "offs": striped(slot_token),
        "pos1": striped(pos[0]),
        "pos2": striped(pos[1]),
        "pos3": striped(pos[2]),
        "pos4": striped(pos[3]),
    }


def reference(xT, w, b, gate, offs, pos1, pos2, pos3, pos4):
    idx = unstriped(offs)
    xq = mxq(f64(xT)[:, idx], 0, "e4m3")
    y = by_expert(mxq(f64(w), 1, "e4m3"), xq)
    y = y + np.repeat(f64(b), C, axis=1)
    return sum(f64(gate[r]) * y[:, unstriped(p)] for r, p in enumerate((pos1, pos2, pos3, pos4)))

@@ -1,0 +1,205 @@
+from contextlib import ExitStack
+
+import concourse.mybir as mybir
+
+K, T, E, C, N = 512, 768, 24, 128, 384
+TOP = 4
+SLOTS = E * C
+P = 128
+PACK = 4
+FLOPS = 2 * K * N * SLOTS
+
+F32 = mybir.dt.float32
+BF16 = mybir.dt.bfloat16
+U32 = mybir.dt.uint32
+U16 = mybir.dt.uint16
+U8 = mybir.dt.uint8
+FP8X4 = mybir.dt.float8_e4m3fn_x4
+MULT = mybir.AluOpType.mult
+IDENTITY = mybir.ActivationFunctionType.Identity
+
+BANDS = N // P
+X_CHUNK = 256
+GATHER = 512
+
+VECTOR_PIECES = (16, 18, 20, 22)
+
+
+def interleave(engine_copy, grouped, raw):
+    engine_copy(
+        out=grouped[:].rearrange("p (c i) j -> p c j i", i=4),
+        in_=raw[:].rearrange("p j (c i) -> p c j i", i=4),
+    )
+
+
+def tile_moe_tk_lin_bias_kernel(tc, xT, w, b, gate, offs, pos1, pos2, pos3, pos4, out):
+    nc = tc.nc
+    with ExitStack() as ctx:
+        lists = ctx.enter_context(tc.tile_pool(name="lists", bufs=1))
+        keep = ctx.enter_context(tc.tile_pool(name="keep", bufs=1))
+        stage = ctx.enter_context(tc.tile_pool(name="stage", bufs=12))
+        work = ctx.enter_context(tc.tile_pool(name="work", bufs=8))
+        gates = ctx.enter_context(tc.tile_pool(name="gates", bufs=12))
+        sums = ctx.enter_context(tc.tile_pool(name="sums", bufs=1))
+        psum = ctx.enter_context(tc.psum_pool(name="psum", bufs=8))
+
+        offs_sb = lists.tile([P, SLOTS // 16], U16, name="offs_sb")
+        pos_sb = [lists.tile([P, T // 16], U16, name=f"pos{r}_sb") for r in range(TOP)]
+        bias = keep.tile([P, BANDS, E], F32, name="bias")
+        x_words = keep.tile([P, T], U32, name="x_words", align_bytes=64)
+        x_bytes = keep.tile([P, T], U8, name="x_bytes", align_bytes=64)
+        slot_words = keep.tile([P, SLOTS], U32, name="slot_words", align_bytes=64)
+        slot_bytes = keep.tile([P, SLOTS], U8, name="slot_bytes", align_bytes=64)
+        y = [keep.tile([P, SLOTS], F32, name=f"y{m}") for m in range(BANDS)]
+
+        HALF = 16
+        order = [(e, 0, 2) for e in range(HALF)] + [(e, 0, 1) for e in range(HALF, E)]
+        order += [(e, 1, 2) for e in range(HALF, E)] + [(e, 2, 1) for e in range(HALF)]
+
+        def load(i):
+            e, m0, bands = order[i]
+            raw = stage.tile([P, PACK, bands * P], F32, name=f"raw{bands}")
+            nc.sync.dma_start(raw[:], w[e].rearrange("(p j) n -> p j n", j=PACK)[:, :, m0 * P : (m0 + bands) * P])
+            return raw
+
+        nc.gpsimd.memset(x_bytes[:], 0)
+        raws = {0: load(0)}
+        nc.sync.dma_start(offs_sb[:], offs)
+        x_rows = xT.rearrange("(p j) t -> p j t", j=PACK)
+        x_raw = []
+        for c in range(T // X_CHUNK):
+            raw = keep.tile([P, PACK, X_CHUNK], F32, name=f"x_raw{c}")
+            nc.sync.dma_start(raw[:], x_rows[:, :, c * X_CHUNK : (c + 1) * X_CHUNK])
+            x_raw.append(raw)
+        nc.sync.dma_start(bias[:], b.rearrange("(m p) e -> p m e", p=P))
+
+        for c in range(T // X_CHUNK):
+            tokens = slice(c * X_CHUNK, (c + 1) * X_CHUNK)
+            grouped = keep.tile([P, X_CHUNK, PACK], BF16, name=f"x_grouped{c}", align_bytes=64)
+            interleave(nc.vector.tensor_copy, grouped, x_raw[c])
+            nc.vector.quantize_mx(
+                out=x_words[:, tokens].bitcast(FP8X4),
+                scales=x_bytes[:, tokens],
+                in_=grouped[:].rearrange("p c j -> p (c j)"),
+            )
+
+        def gather(g, table, slots):
+            s = slice(g * GATHER, (g + 1) * GATHER)
+            o = offs_sb[:, g * GATHER // 16 : (g + 1) * GATHER // 16]
+            nc.vector.tensor_copy(slots[:, s], table[:].indirect(o))
+
+        def copy(i, raw):
+            grouped = work.tile([P, order[i][2] * P, PACK], BF16, name="grouped", align_bytes=64)
+            interleave(nc.vector.tensor_copy if i in VECTOR_PIECES else nc.scalar.copy, grouped, raw)
+            return grouped
+
+        def quantize(i, grouped):
+            width = order[i][2] * P
+            words = work.tile([P, width], U32, name="words", align_bytes=64)
+            scales = work.tile([P, width], U8, name="scales", align_bytes=64)
+            nc.vector.quantize_mx(
+                out=words[:].bitcast(FP8X4), scales=scales[:], in_=grouped[:].rearrange("p n j -> p (n j)")
+            )
+            return words, scales
+
+        def multiply(i, words, scales):
+            e, m0, bands = order[i]
+            s = slice(e * C, (e + 1) * C)
+            bank = psum.tile([P, bands, C], F32, name="bank")
+            for q in range(bands):
+                rows = slice(q * P, (q + 1) * P)
+                nc.tensor.matmul_mx(
+                    out=bank[:, q, :],
+                    lhsT=words[:, rows].bitcast(FP8X4),
+                    lhsT_scale=scales[:, rows],
+                    rhs=slot_words[:, s].bitcast(FP8X4),
+                    rhs_scale=slot_bytes[:, s],
+                    start=True,
+                    stop=True,
+                )
+            return bank
+
+        def empty(i, bank):
+            e, m0, bands = order[i]
+            for q in range(bands):
+                m = m0 + q
+                nc.scalar.activation(
+                    y[m][:, e * C : (e + 1) * C], bank[:, q, :], IDENTITY, bias=bias[:, m, e : e + 1]
+                )
+
+        def load_gates(m):
+            tiles = []
+            for r in range(TOP):
+                g = gates.tile([P, T], F32, name="g")
+                nc.sync.dma_start(g[:], gate[r, m * P : (m + 1) * P, :])
+                tiles.append(g)
+            return tiles
+
+        def combine(m, g):
+            H = T // 2
+            lo, hi = slice(0, H), slice(H, T)
+            held = {}
+
+            def at(name):
+                if name not in held:
+                    held[name] = sums.tile([P, T], F32, name=name)
+                return held[name]
+
+            def fetch(r, c):
+                o = pos_sb[r][:] if c is None else pos_sb[r][:, c.start // 16 : c.stop // 16]
+                c = c or slice(0, T)
+                nc.vector.tensor_tensor(at(f"prod{r}")[:, c], y[m][:].indirect(o), g[r][:, c], MULT)
+
+            def finish(c):
+                nc.vector.tensor_add(at("total")[:, c], at("second")[:, c], at("prod3")[:, c])
+                (nc.sync if m == BANDS - 1 else nc.gpsimd).dma_start(out[m * P : (m + 1) * P, c], at("total")[:, c])
+
+            return [
+                lambda: fetch(0, None),
+                lambda: fetch(1, None),
+                lambda: fetch(2, None),
+                lambda: nc.vector.tensor_add(at("first")[:], at("prod0")[:], at("prod1")[:]),
+                lambda: fetch(3, lo),
+                lambda: nc.vector.tensor_add(at("second")[:], at("first")[:], at("prod2")[:]),
+                lambda: fetch(3, hi),
+                lambda: finish(lo),
+                lambda: finish(hi),
+            ]
+
+        g = {}
+        groups, codes, banks = {}, {}, {}
+        vector_steps = []
+        for k in range(SLOTS // GATHER):
+            vector_steps.append(lambda k=k: gather(k, x_words, slot_words))
+            vector_steps.append(lambda k=k: gather(k, x_bytes, slot_bytes))
+        LAST = len(order)
+        QL, ML, EL = 2, 3, 4
+        for i in range(LAST):
+            if i == E - 4:
+                for r, pos in enumerate((pos1, pos2, pos3, pos4)):
+                    nc.sync.dma_start(pos_sb[r][:], pos)
+                g[0] = load_gates(0)
+            if i == E + (E - HALF) - 3:
+                g[1] = load_gates(1)
+            if i > 0:
+                raws[i] = load(i)
+        g[2] = load_gates(2)
+        for s in range(4):
+            vector_steps.pop(0)()
+        for i in range(LAST + EL + 1):
+            if i < LAST:
+                groups[i] = copy(i, raws[i])
+            if 0 <= i - QL < LAST:
+                codes[i - QL] = quantize(i - QL, groups[i - QL])
+            if 0 <= i - ML < LAST:
+                banks[i - ML] = multiply(i - ML, *codes[i - ML])
+            if 0 <= i - EL < LAST:
+                empty(i - EL, banks[i - EL])
+            if i - EL == E - 1:
+                vector_steps += combine(0, g[0])
+            if i - EL == E + (E - HALF) - 1:
+                vector_steps += combine(1, g[1])
+            if i > 0 and vector_steps:
+                vector_steps.pop(0)()
+        for step in vector_steps + combine(2, g[2]):
+            step()

@@ -11,6 +11,7 @@ FLOPS = 2 * K * N * SLOTS
 
 F32 = mybir.dt.float32
 BF16 = mybir.dt.bfloat16
+I32 = mybir.dt.int32
 U32 = mybir.dt.uint32
 U16 = mybir.dt.uint16
 U8 = mybir.dt.uint8
@@ -19,16 +20,16 @@ MULT = mybir.AluOpType.mult
 IDENTITY = mybir.ActivationFunctionType.Identity
 
 BANDS = N // P
-X_CHUNK = 256
 GATHER = 512
-
-VECTOR_PIECES = (16, 18, 20, 22)
+WHOLE = 12
+QL, ML, EL = 2, 3, 10
+VECTOR_COPIES = (1, 5, 9, 13, 17, 21)
 
 
 def interleave(engine_copy, grouped, raw):
     engine_copy(
         out=grouped[:].rearrange("p (c i) j -> p c j i", i=4),
-        in_=raw[:].rearrange("p j (c i) -> p c j i", i=4),
+        in_=raw.rearrange("p j (c i) -> p c j i", i=4),
     )
 
 
@@ -37,9 +38,12 @@ def tile_moe_tk_lin_bias_kernel(tc, xT, w, b, gate, offs, pos1, pos2, pos3, pos4
     with ExitStack() as ctx:
         lists = ctx.enter_context(tc.tile_pool(name="lists", bufs=1))
         keep = ctx.enter_context(tc.tile_pool(name="keep", bufs=1))
-        stage = ctx.enter_context(tc.tile_pool(name="stage", bufs=12))
-        work = ctx.enter_context(tc.tile_pool(name="work", bufs=8))
-        gates = ctx.enter_context(tc.tile_pool(name="gates", bufs=12))
+        stage = ctx.enter_context(tc.tile_pool(name="stage", bufs=19))
+        wide = ctx.enter_context(tc.tile_pool(name="wide", bufs=12))
+        narrow = ctx.enter_context(tc.tile_pool(name="narrow", bufs=6))
+        wide_codes = ctx.enter_context(tc.tile_pool(name="wide_codes", bufs=4))
+        narrow_codes = ctx.enter_context(tc.tile_pool(name="narrow_codes", bufs=4))
+        slots = ctx.enter_context(tc.tile_pool(name="slots", bufs=3))
         sums = ctx.enter_context(tc.tile_pool(name="sums", bufs=1))
         psum = ctx.enter_context(tc.psum_pool(name="psum", bufs=8))
 
@@ -48,94 +52,127 @@ def tile_moe_tk_lin_bias_kernel(tc, xT, w, b, gate, offs, pos1, pos2, pos3, pos4
         bias = keep.tile([P, BANDS, E], F32, name="bias")
         x_words = keep.tile([P, T], U32, name="x_words", align_bytes=64)
         x_bytes = keep.tile([P, T], U8, name="x_bytes", align_bytes=64)
-        slot_words = keep.tile([P, SLOTS], U32, name="slot_words", align_bytes=64)
-        slot_bytes = keep.tile([P, SLOTS], U8, name="slot_bytes", align_bytes=64)
         y = [keep.tile([P, SLOTS], F32, name=f"y{m}") for m in range(BANDS)]
 
-        HALF = 16
-        order = [(e, 0, 2) for e in range(HALF)] + [(e, 0, 1) for e in range(HALF, E)]
-        order += [(e, 1, 2) for e in range(HALF, E)] + [(e, 2, 1) for e in range(HALF)]
-
-        def load(i):
-            e, m0, bands = order[i]
-            raw = stage.tile([P, PACK, bands * P], F32, name=f"raw{bands}")
-            nc.sync.dma_start(raw[:], w[e].rearrange("(p j) n -> p j n", j=PACK)[:, :, m0 * P : (m0 + bands) * P])
+        def load_whole(source):
+            raw = stage.tile([P, PACK, N], F32, name="raw")
+            nc.sync.dma_start(raw[:], source)
             return raw
 
-        nc.gpsimd.memset(x_bytes[:], 0)
-        raws = {0: load(0)}
-        nc.sync.dma_start(offs_sb[:], offs)
-        x_rows = xT.rearrange("(p j) t -> p j t", j=PACK)
-        x_raw = []
-        for c in range(T // X_CHUNK):
-            raw = keep.tile([P, PACK, X_CHUNK], F32, name=f"x_raw{c}")
-            nc.sync.dma_start(raw[:], x_rows[:, :, c * X_CHUNK : (c + 1) * X_CHUNK])
-            x_raw.append(raw)
-        nc.sync.dma_start(bias[:], b.rearrange("(m p) e -> p m e", p=P))
+        def load_three(e, m):
+            raw = stage.tile([P, PACK, N], F32, name="raw")
+            for h in range(3):
+                nc.sync.dma_start(raw[:, :, h * P : (h + 1) * P], w_rows(e + h)[:, :, m * P : (m + 1) * P])
+            return raw
 
-        for c in range(T // X_CHUNK):
-            tokens = slice(c * X_CHUNK, (c + 1) * X_CHUNK)
-            grouped = keep.tile([P, X_CHUNK, PACK], BF16, name=f"x_grouped{c}", align_bytes=64)
-            interleave(nc.vector.tensor_copy, grouped, x_raw[c])
-            nc.vector.quantize_mx(
-                out=x_words[:, tokens].bitcast(FP8X4),
-                scales=x_bytes[:, tokens],
-                in_=grouped[:].rearrange("p c j -> p (c j)"),
-            )
+        def w_rows(e):
+            return w[e].rearrange("(p j) n -> p j n", j=PACK)
 
-        def gather(g, table, slots):
-            s = slice(g * GATHER, (g + 1) * GATHER)
-            o = offs_sb[:, g * GATHER // 16 : (g + 1) * GATHER // 16]
-            nc.vector.tensor_copy(slots[:, s], table[:].indirect(o))
-
-        def copy(i, raw):
-            grouped = work.tile([P, order[i][2] * P, PACK], BF16, name="grouped", align_bytes=64)
-            interleave(nc.vector.tensor_copy if i in VECTOR_PIECES else nc.scalar.copy, grouped, raw)
+        def group(engine_copy, raw, width):
+            pool = wide if width == 2 * P else narrow
+            grouped = pool.tile([P, width, PACK], BF16, name="grouped", align_bytes=64)
+            interleave(engine_copy, grouped, raw)
             return grouped
 
-        def quantize(i, grouped):
-            width = order[i][2] * P
-            words = work.tile([P, width], U32, name="words", align_bytes=64)
-            scales = work.tile([P, width], U8, name="scales", align_bytes=64)
+        def quantize(words, scales, grouped):
             nc.vector.quantize_mx(
-                out=words[:].bitcast(FP8X4), scales=scales[:], in_=grouped[:].rearrange("p n j -> p (n j)")
+                out=words.bitcast(FP8X4), scales=scales, in_=grouped[:].rearrange("p c j -> p (c j)")
             )
+
+        slot_words, slot_bytes = {}, {}
+
+        def gather_words(k):
+            slot_words[k] = slots.tile([P, GATHER], U32, name="slot_words", align_bytes=64)
+            nc.vector.tensor_copy(slot_words[k][:], x_words[:].indirect(offs_sb[:, k * 32 : (k + 1) * 32]))
+
+        def gather_bytes(k):
+            slot_bytes[k] = slots.tile([P, GATHER], U8, name="slot_bytes", align_bytes=64)
+            nc.vector.tensor_copy(slot_bytes[k][:], x_bytes[:].indirect(offs_sb[:, k * 32 : (k + 1) * 32]))
+
+        nc.gpsimd.memset(x_bytes[:], 0)
+        x_rows = xT.rearrange("(p j) t -> p j t", j=PACK)
+        raw_of = {}
+        raw_of[0] = load_whole(w_rows(0))
+        x_raw = []
+        for h in range(T // N):
+            x_raw.append(load_whole(x_rows[:, :, h * N : (h + 1) * N]))
+            if h == 0:
+                nc.sync.dma_start(offs_sb[:], offs)
+        nc.sync.dma_start(bias[:], b.rearrange("(m p) e -> p m e", p=P))
+        for e in range(1, WHOLE):
+            raw_of[e] = load_whole(w_rows(e))
+
+        def load_gates(m):
+            rows = []
+            for r in range(0, TOP, 2):
+                pair = stage.tile([P, 2, T], F32, name="raw")
+                for h in range(2):
+                    nc.sync.dma_start(pair[:, h, :], gate[r + h, m * P : (m + 1) * P, :])
+                    rows.append(pair[:, h, :])
+            return rows
+
+        g = []
+        for m in range(BANDS):
+            for e in range(WHOLE, E, 3):
+                raw_of[e, m] = load_three(e, m)
+            if m == 0:
+                for r, pos in enumerate((pos1, pos2, pos3, pos4)):
+                    nc.sync.dma_start(pos_sb[r][:], pos)
+            g.append(load_gates(m))
+
+        for h in range(T // N):
+            for n0, width in ((0, 2 * P), (2 * P, P)):
+                tokens = slice(h * N + n0, h * N + n0 + width)
+                grouped = group(nc.vector.tensor_copy, x_raw[h][:, :, n0 : n0 + width], width)
+                quantize(x_words[:, tokens], x_bytes[:, tokens], grouped)
+
+        units = []
+        for e in range(WHOLE):
+            units.append([(e, 0), (e, 1)])
+            units.append([(e, 2)])
+        for m in range(BANDS):
+            for e in range(WHOLE, E, 3):
+                units.append([(e, m), (e + 1, m)])
+                units.append([(e + 2, m)])
+
+        def copy_unit(i):
+            (e, m), width = units[i][0], len(units[i]) * P
+            if e < WHOLE:
+                raw, n0 = raw_of[e], m * P
+            else:
+                raw, n0 = raw_of[e - (e - WHOLE) % 3, m], (e - WHOLE) % 3 * P
+            return group(nc.vector.tensor_copy if i in VECTOR_COPIES else nc.scalar.copy, raw[:, :, n0 : n0 + width], width)
+
+        def quantize_unit(u, grouped):
+            pool = wide_codes if len(u) == 2 else narrow_codes
+            words = pool.tile([P, len(u) * P], U32, name="words", align_bytes=64)
+            scales = pool.tile([P, len(u) * P], U8, name="scales", align_bytes=64)
+            quantize(words[:], scales[:], grouped)
             return words, scales
 
-        def multiply(i, words, scales):
-            e, m0, bands = order[i]
-            s = slice(e * C, (e + 1) * C)
-            bank = psum.tile([P, bands, C], F32, name="bank")
-            for q in range(bands):
+        def multiply(u, words, scales):
+            bank = psum.tile([P, len(u), C], F32, name="bank")
+            for q, (e, m) in enumerate(u):
                 rows = slice(q * P, (q + 1) * P)
+                k, s = e // 4, slice(e % 4 * C, (e % 4 + 1) * C)
                 nc.tensor.matmul_mx(
                     out=bank[:, q, :],
                     lhsT=words[:, rows].bitcast(FP8X4),
                     lhsT_scale=scales[:, rows],
-                    rhs=slot_words[:, s].bitcast(FP8X4),
-                    rhs_scale=slot_bytes[:, s],
+                    rhs=slot_words[k][:, s].bitcast(FP8X4),
+                    rhs_scale=slot_bytes[k][:, s],
                     start=True,
                     stop=True,
                 )
             return bank
 
-        def empty(i, bank):
-            e, m0, bands = order[i]
-            for q in range(bands):
-                m = m0 + q
+        def empty(u, bank):
+            for q, (e, m) in enumerate(u):
                 nc.scalar.activation(
                     y[m][:, e * C : (e + 1) * C], bank[:, q, :], IDENTITY, bias=bias[:, m, e : e + 1]
                 )
 
-        def load_gates(m):
-            tiles = []
-            for r in range(TOP):
-                g = gates.tile([P, T], F32, name="g")
-                nc.sync.dma_start(g[:], gate[r, m * P : (m + 1) * P, :])
-                tiles.append(g)
-            return tiles
-
-        def combine(m, g):
+        def combine(m):
             H = T // 2
             lo, hi = slice(0, H), slice(H, T)
             held = {}
@@ -148,58 +185,44 @@ def tile_moe_tk_lin_bias_kernel(tc, xT, w, b, gate, offs, pos1, pos2, pos3, pos4
             def fetch(r, c):
                 o = pos_sb[r][:] if c is None else pos_sb[r][:, c.start // 16 : c.stop // 16]
                 c = c or slice(0, T)
-                nc.vector.tensor_tensor(at(f"prod{r}")[:, c], y[m][:].indirect(o), g[r][:, c], MULT)
+                nc.vector.tensor_tensor(at(f"prod{r}")[:, c], y[m][:].indirect(o), g[m][r][:, c], MULT)
 
             def finish(c):
                 nc.vector.tensor_add(at("total")[:, c], at("second")[:, c], at("prod3")[:, c])
                 (nc.sync if m == BANDS - 1 else nc.gpsimd).dma_start(out[m * P : (m + 1) * P, c], at("total")[:, c])
 
-            return [
+            start = [
                 lambda: fetch(0, None),
                 lambda: fetch(1, None),
                 lambda: fetch(2, None),
                 lambda: nc.vector.tensor_add(at("first")[:], at("prod0")[:], at("prod1")[:]),
-                lambda: fetch(3, lo),
-                lambda: nc.vector.tensor_add(at("second")[:], at("first")[:], at("prod2")[:]),
-                lambda: fetch(3, hi),
-                lambda: finish(lo),
-                lambda: finish(hi),
             ]
+            add = [lambda: nc.vector.tensor_add(at("second")[:], at("first")[:], at("prod2")[:])]
+            if m < BANDS - 1:
+                return start + [lambda: fetch(3, None)] + add + [lambda: finish(slice(0, T))]
+            return start + [lambda: fetch(3, lo)] + add + [lambda: fetch(3, hi), lambda: finish(lo), lambda: finish(hi)]
 
-        g = {}
         groups, codes, banks = {}, {}, {}
-        vector_steps = []
+        steps = []
         for k in range(SLOTS // GATHER):
-            vector_steps.append(lambda k=k: gather(k, x_words, slot_words))
-            vector_steps.append(lambda k=k: gather(k, x_bytes, slot_bytes))
-        LAST = len(order)
-        QL, ML, EL = 2, 3, 4
-        for i in range(LAST):
-            if i == E - 4:
-                for r, pos in enumerate((pos1, pos2, pos3, pos4)):
-                    nc.sync.dma_start(pos_sb[r][:], pos)
-                g[0] = load_gates(0)
-            if i == E + (E - HALF) - 3:
-                g[1] = load_gates(1)
-            if i > 0:
-                raws[i] = load(i)
-        g[2] = load_gates(2)
-        for s in range(4):
-            vector_steps.pop(0)()
-        for i in range(LAST + EL + 1):
-            if i < LAST:
-                groups[i] = copy(i, raws[i])
-            if 0 <= i - QL < LAST:
-                codes[i - QL] = quantize(i - QL, groups[i - QL])
-            if 0 <= i - ML < LAST:
-                banks[i - ML] = multiply(i - ML, *codes[i - ML])
-            if 0 <= i - EL < LAST:
-                empty(i - EL, banks[i - EL])
-            if i - EL == E - 1:
-                vector_steps += combine(0, g[0])
-            if i - EL == E + (E - HALF) - 1:
-                vector_steps += combine(1, g[1])
-            if i > 0 and vector_steps:
-                vector_steps.pop(0)()
-        for step in vector_steps + combine(2, g[2]):
+            steps.append(lambda k=k: gather_words(k))
+            steps.append(lambda k=k: gather_bytes(k))
+        for s in range(2):
+            steps.pop(0)()
+        last = len(units)
+        for i in range(last + EL):
+            if i < last:
+                groups[i] = copy_unit(i)
+            if 0 <= i - QL < last:
+                codes[i - QL] = quantize_unit(units[i - QL], groups[i - QL])
+            if 0 <= i - ML < last:
+                banks[i - ML] = multiply(units[i - ML], *codes[i - ML])
+            if 0 <= i - EL < last:
+                empty(units[i - EL], banks[i - EL])
+            for m in range(BANDS - 1):
+                if i - EL == 2 * WHOLE + (m + 1) * (E - WHOLE) * 2 // 3 - 1:
+                    steps += combine(m)
+            if i > 0 and steps and (i % 2 == 0 or i >= 2 * WHOLE):
+                steps.pop(0)()
+        for step in steps + combine(BANDS - 1):
             step()

@@ -11,26 +11,19 @@ FLOPS = 2 * K * N * SLOTS
 
 F32 = mybir.dt.float32
 BF16 = mybir.dt.bfloat16
-I32 = mybir.dt.int32
 U32 = mybir.dt.uint32
 U16 = mybir.dt.uint16
 U8 = mybir.dt.uint8
 FP8X4 = mybir.dt.float8_e4m3fn_x4
-MULT = mybir.AluOpType.mult
+ADD, MULT = mybir.AluOpType.add, mybir.AluOpType.mult
 IDENTITY = mybir.ActivationFunctionType.Identity
 
 BANDS = N // P
-GATHER = 512
-WHOLE = 12
-QL, ML, EL = 2, 3, 10
-VECTOR_COPIES = (1, 5, 9, 13, 17, 21)
-
-
-def interleave(engine_copy, grouped, raw):
-    engine_copy(
-        out=grouped[:].rearrange("p (c i) j -> p c j i", i=4),
-        in_=raw.rearrange("p j (c i) -> p c j i", i=4),
-    )
+TEAM = 4
+GATHER = TEAM * C
+PARTS = ((0, 2 * P), (2 * P, P))
+VECTOR_NARROW = ()
+SCALAR_TEAMS = (5,)
 
 
 def tile_moe_tk_lin_bias_kernel(tc, xT, w, b, gate, offs, pos1, pos2, pos3, pos4, out):
@@ -38,11 +31,10 @@ def tile_moe_tk_lin_bias_kernel(tc, xT, w, b, gate, offs, pos1, pos2, pos3, pos4
     with ExitStack() as ctx:
         lists = ctx.enter_context(tc.tile_pool(name="lists", bufs=1))
         keep = ctx.enter_context(tc.tile_pool(name="keep", bufs=1))
-        stage = ctx.enter_context(tc.tile_pool(name="stage", bufs=19))
-        wide = ctx.enter_context(tc.tile_pool(name="wide", bufs=12))
+        stage = ctx.enter_context(tc.tile_pool(name="stage", bufs=20))
+        wide = ctx.enter_context(tc.tile_pool(name="wide", bufs=8))
         narrow = ctx.enter_context(tc.tile_pool(name="narrow", bufs=6))
-        wide_codes = ctx.enter_context(tc.tile_pool(name="wide_codes", bufs=4))
-        narrow_codes = ctx.enter_context(tc.tile_pool(name="narrow_codes", bufs=4))
+        codes = ctx.enter_context(tc.tile_pool(name="codes", bufs=4))
         slots = ctx.enter_context(tc.tile_pool(name="slots", bufs=3))
         sums = ctx.enter_context(tc.tile_pool(name="sums", bufs=1))
         psum = ctx.enter_context(tc.psum_pool(name="psum", bufs=8))
@@ -54,24 +46,32 @@ def tile_moe_tk_lin_bias_kernel(tc, xT, w, b, gate, offs, pos1, pos2, pos3, pos4
         x_bytes = keep.tile([P, T], U8, name="x_bytes", align_bytes=64)
         y = [keep.tile([P, SLOTS], F32, name=f"y{m}") for m in range(BANDS)]
 
-        def load_whole(source):
+        def load(source):
             raw = stage.tile([P, PACK, N], F32, name="raw")
-            nc.sync.dma_start(raw[:], source)
+            nc.sync.dma_start(raw[:], source.rearrange("(p j) c -> p j c", j=PACK))
             return raw
 
-        def load_three(e, m):
-            raw = stage.tile([P, PACK, N], F32, name="raw")
-            for h in range(3):
-                nc.sync.dma_start(raw[:, :, h * P : (h + 1) * P], w_rows(e + h)[:, :, m * P : (m + 1) * P])
-            return raw
+        nc.gpsimd.memset(x_bytes[:], 0)
+        x_raw = [load(xT[:, :N])]
+        nc.sync.dma_start(offs_sb[:], offs)
+        x_raw.append(load(xT[:, N:]))
+        w_raw = [load(w[0])]
+        nc.sync.dma_start(bias[:], b.rearrange("(m p) e -> p m e", p=P))
+        for e in range(1, E):
+            w_raw.append(load(w[e]))
+        for pos_tile, pos in zip(pos_sb, (pos1, pos2, pos3, pos4)):
+            nc.sync.dma_start(pos_tile[:], pos)
+        gates = []
+        for m in range(BANDS):
+            for r in range(TOP):
+                if r % 2 == 0:
+                    pair = stage.tile([P, 2, T], F32, name="raw")
+                nc.sync.dma_start(pair[:, r % 2, :], gate[r, m * P : (m + 1) * P, :])
+                gates.append(pair[:, r % 2, :])
 
-        def w_rows(e):
-            return w[e].rearrange("(p j) n -> p j n", j=PACK)
-
-        def group(engine_copy, raw, width):
-            pool = wide if width == 2 * P else narrow
-            grouped = pool.tile([P, width, PACK], BF16, name="grouped", align_bytes=64)
-            interleave(engine_copy, grouped, raw)
+        def group(copy, raw, start, width):
+            grouped = (wide if width == 2 * P else narrow).tile([P, width, PACK], BF16, name="grouped", align_bytes=64)
+            copy(out=grouped[:], in_=raw[:, :, start : start + width].rearrange("p j c -> p c j"))
             return grouped
 
         def quantize(words, scales, grouped):
@@ -79,150 +79,75 @@ def tile_moe_tk_lin_bias_kernel(tc, xT, w, b, gate, offs, pos1, pos2, pos3, pos4
                 out=words.bitcast(FP8X4), scales=scales, in_=grouped[:].rearrange("p c j -> p (c j)")
             )
 
-        slot_words, slot_bytes = {}, {}
-
-        def gather_words(k):
-            slot_words[k] = slots.tile([P, GATHER], U32, name="slot_words", align_bytes=64)
-            nc.vector.tensor_copy(slot_words[k][:], x_words[:].indirect(offs_sb[:, k * 32 : (k + 1) * 32]))
-
-        def gather_bytes(k):
-            slot_bytes[k] = slots.tile([P, GATHER], U8, name="slot_bytes", align_bytes=64)
-            nc.vector.tensor_copy(slot_bytes[k][:], x_bytes[:].indirect(offs_sb[:, k * 32 : (k + 1) * 32]))
-
-        nc.gpsimd.memset(x_bytes[:], 0)
-        x_rows = xT.rearrange("(p j) t -> p j t", j=PACK)
-        raw_of = {}
-        raw_of[0] = load_whole(w_rows(0))
-        x_raw = []
-        for h in range(T // N):
-            x_raw.append(load_whole(x_rows[:, :, h * N : (h + 1) * N]))
-            if h == 0:
-                nc.sync.dma_start(offs_sb[:], offs)
-        nc.sync.dma_start(bias[:], b.rearrange("(m p) e -> p m e", p=P))
-        for e in range(1, WHOLE):
-            raw_of[e] = load_whole(w_rows(e))
-
-        def load_gates(m):
-            rows = []
-            for r in range(0, TOP, 2):
-                pair = stage.tile([P, 2, T], F32, name="raw")
-                for h in range(2):
-                    nc.sync.dma_start(pair[:, h, :], gate[r + h, m * P : (m + 1) * P, :])
-                    rows.append(pair[:, h, :])
-            return rows
-
-        g = []
-        for m in range(BANDS):
-            for e in range(WHOLE, E, 3):
-                raw_of[e, m] = load_three(e, m)
-            if m == 0:
-                for r, pos in enumerate((pos1, pos2, pos3, pos4)):
-                    nc.sync.dma_start(pos_sb[r][:], pos)
-            g.append(load_gates(m))
-
-        for h in range(T // N):
-            for n0, width in ((0, 2 * P), (2 * P, P)):
-                tokens = slice(h * N + n0, h * N + n0 + width)
-                grouped = group(nc.vector.tensor_copy, x_raw[h][:, :, n0 : n0 + width], width)
+        for h in range(2):
+            for start, width in PARTS:
+                tokens = slice(h * N + start, h * N + start + width)
+                grouped = group(nc.vector.tensor_copy, x_raw[h], start, width)
                 quantize(x_words[:, tokens], x_bytes[:, tokens], grouped)
 
-        units = []
-        for e in range(WHOLE):
-            units.append([(e, 0), (e, 1)])
-            units.append([(e, 2)])
+        for team in range(E // TEAM):
+            o = offs_sb[:, team * GATHER // 16 : (team + 1) * GATHER // 16]
+            slot_words = slots.tile([P, GATHER], U32, name="slot_words", align_bytes=64)
+            nc.vector.tensor_copy(slot_words[:], x_words[:].indirect(o))
+            slot_bytes = slots.tile([P, GATHER], U8, name="slot_bytes", align_bytes=64)
+            nc.vector.tensor_copy(slot_bytes[:], x_bytes[:].indirect(o))
+            banks = [psum.tile([P, TEAM, C], F32, name="bank") for m in range(BANDS)]
+            for q in range(TEAM):
+                e = team * TEAM + q
+                s = slice(q * C, (q + 1) * C)
+                words = codes.tile([P, N], U32, name="words", align_bytes=64)
+                scales = codes.tile([P, N], U8, name="scales", align_bytes=64)
+                for start, width in PARTS:
+                    on_vector = width == P and e in VECTOR_NARROW
+                    grouped = group(nc.vector.tensor_copy if on_vector else nc.scalar.copy, w_raw[e], start, width)
+                    quantize(words[:, start : start + width], scales[:, start : start + width], grouped)
+                for m in range(BANDS):
+                    rows = slice(m * P, (m + 1) * P)
+                    nc.tensor.matmul_mx(
+                        out=banks[m][:, q, :],
+                        lhsT=words[:, rows].bitcast(FP8X4),
+                        lhsT_scale=scales[:, rows],
+                        rhs=slot_words[:, s].bitcast(FP8X4),
+                        rhs_scale=slot_bytes[:, s],
+                        start=True,
+                        stop=True,
+                    )
+            experts = slice(team * TEAM, (team + 1) * TEAM)
+            for m in range(BANDS):
+                if team in SCALAR_TEAMS:
+                    for q in range(TEAM):
+                        e = team * TEAM + q
+                        nc.scalar.activation(
+                            y[m][:, e * C : (e + 1) * C], banks[m][:, q, :], IDENTITY, bias=bias[:, m, e : e + 1]
+                        )
+                else:
+                    nc.vector.tensor_tensor(
+                        y[m][:, team * GATHER : (team + 1) * GATHER].rearrange("p (q c) -> p q c", q=TEAM),
+                        banks[m][:],
+                        bias[:, m, experts].unsqueeze(2).to_broadcast([P, TEAM, C]),
+                        ADD,
+                    )
+
+        H = T // 2
+        lo, hi = slice(0, H), slice(H, T)
         for m in range(BANDS):
-            for e in range(WHOLE, E, 3):
-                units.append([(e, m), (e + 1, m)])
-                units.append([(e + 2, m)])
-
-        def copy_unit(i):
-            (e, m), width = units[i][0], len(units[i]) * P
-            if e < WHOLE:
-                raw, n0 = raw_of[e], m * P
-            else:
-                raw, n0 = raw_of[e - (e - WHOLE) % 3, m], (e - WHOLE) % 3 * P
-            return group(nc.vector.tensor_copy if i in VECTOR_COPIES else nc.scalar.copy, raw[:, :, n0 : n0 + width], width)
-
-        def quantize_unit(u, grouped):
-            pool = wide_codes if len(u) == 2 else narrow_codes
-            words = pool.tile([P, len(u) * P], U32, name="words", align_bytes=64)
-            scales = pool.tile([P, len(u) * P], U8, name="scales", align_bytes=64)
-            quantize(words[:], scales[:], grouped)
-            return words, scales
-
-        def multiply(u, words, scales):
-            bank = psum.tile([P, len(u), C], F32, name="bank")
-            for q, (e, m) in enumerate(u):
-                rows = slice(q * P, (q + 1) * P)
-                k, s = e // 4, slice(e % 4 * C, (e % 4 + 1) * C)
-                nc.tensor.matmul_mx(
-                    out=bank[:, q, :],
-                    lhsT=words[:, rows].bitcast(FP8X4),
-                    lhsT_scale=scales[:, rows],
-                    rhs=slot_words[k][:, s].bitcast(FP8X4),
-                    rhs_scale=slot_bytes[k][:, s],
-                    start=True,
-                    stop=True,
-                )
-            return bank
-
-        def empty(u, bank):
-            for q, (e, m) in enumerate(u):
-                nc.scalar.activation(
-                    y[m][:, e * C : (e + 1) * C], bank[:, q, :], IDENTITY, bias=bias[:, m, e : e + 1]
-                )
-
-        def combine(m):
-            H = T // 2
-            lo, hi = slice(0, H), slice(H, T)
-            held = {}
-
-            def at(name):
-                if name not in held:
-                    held[name] = sums.tile([P, T], F32, name=name)
-                return held[name]
+            prod = [sums.tile([P, T], F32, name=f"prod{r}") for r in range(TOP)]
+            first = sums.tile([P, T], F32, name="first")
+            second = sums.tile([P, T], F32, name="second")
+            total = sums.tile([P, T], F32, name="total")
 
             def fetch(r, c):
-                o = pos_sb[r][:] if c is None else pos_sb[r][:, c.start // 16 : c.stop // 16]
-                c = c or slice(0, T)
-                nc.vector.tensor_tensor(at(f"prod{r}")[:, c], y[m][:].indirect(o), g[m][r][:, c], MULT)
+                o = pos_sb[r][:, c.start // 16 : c.stop // 16]
+                nc.vector.tensor_tensor(prod[r][:, c], y[m][:].indirect(o), gates[m * TOP + r][:, c], MULT)
 
-            def finish(c):
-                nc.vector.tensor_add(at("total")[:, c], at("second")[:, c], at("prod3")[:, c])
-                (nc.sync if m == BANDS - 1 else nc.gpsimd).dma_start(out[m * P : (m + 1) * P, c], at("total")[:, c])
-
-            start = [
-                lambda: fetch(0, None),
-                lambda: fetch(1, None),
-                lambda: fetch(2, None),
-                lambda: nc.vector.tensor_add(at("first")[:], at("prod0")[:], at("prod1")[:]),
-            ]
-            add = [lambda: nc.vector.tensor_add(at("second")[:], at("first")[:], at("prod2")[:])]
-            if m < BANDS - 1:
-                return start + [lambda: fetch(3, None)] + add + [lambda: finish(slice(0, T))]
-            return start + [lambda: fetch(3, lo)] + add + [lambda: fetch(3, hi), lambda: finish(lo), lambda: finish(hi)]
-
-        groups, codes, banks = {}, {}, {}
-        steps = []
-        for k in range(SLOTS // GATHER):
-            steps.append(lambda k=k: gather_words(k))
-            steps.append(lambda k=k: gather_bytes(k))
-        for s in range(2):
-            steps.pop(0)()
-        last = len(units)
-        for i in range(last + EL):
-            if i < last:
-                groups[i] = copy_unit(i)
-            if 0 <= i - QL < last:
-                codes[i - QL] = quantize_unit(units[i - QL], groups[i - QL])
-            if 0 <= i - ML < last:
-                banks[i - ML] = multiply(units[i - ML], *codes[i - ML])
-            if 0 <= i - EL < last:
-                empty(units[i - EL], banks[i - EL])
-            for m in range(BANDS - 1):
-                if i - EL == 2 * WHOLE + (m + 1) * (E - WHOLE) * 2 // 3 - 1:
-                    steps += combine(m)
-            if i > 0 and steps and (i % 2 == 0 or i >= 2 * WHOLE):
-                steps.pop(0)()
-        for step in steps + combine(BANDS - 1):
-            step()
+            whole = slice(0, T)
+            fetch(0, whole)
+            fetch(1, whole)
+            fetch(2, whole)
+            nc.vector.tensor_add(first[:], prod[0][:], prod[1][:])
+            fetch(3, lo)
+            nc.vector.tensor_add(second[:], first[:], prod[2][:])
+            fetch(3, hi)
+            for c in (lo, hi):
+                nc.vector.tensor_add(total[:, c], second[:, c], prod[3][:, c])
+                nc.sync.dma_start(out[m * P : (m + 1) * P, c], total[:, c])

@@ -1,6 +1,7 @@
 from contextlib import ExitStack
 
 import concourse.mybir as mybir
+from concourse.masks import make_identity
 
 K, T, E, C, N = 512, 768, 24, 128, 384
 TOP = 4
@@ -22,8 +23,6 @@ BANDS = N // P
 TEAM = 4
 GATHER = TEAM * C
 PARTS = ((0, 2 * P), (2 * P, P))
-VECTOR_NARROW = ()
-SCALAR_TEAMS = (5,)
 
 
 def tile_moe_tk_lin_bias_kernel(tc, xT, w, b, gate, offs, pos1, pos2, pos3, pos4, out):
@@ -31,11 +30,12 @@ def tile_moe_tk_lin_bias_kernel(tc, xT, w, b, gate, offs, pos1, pos2, pos3, pos4
     with ExitStack() as ctx:
         lists = ctx.enter_context(tc.tile_pool(name="lists", bufs=1))
         keep = ctx.enter_context(tc.tile_pool(name="keep", bufs=1))
-        stage = ctx.enter_context(tc.tile_pool(name="stage", bufs=20))
+        stage = ctx.enter_context(tc.tile_pool(name="stage", bufs=18))
         wide = ctx.enter_context(tc.tile_pool(name="wide", bufs=8))
         narrow = ctx.enter_context(tc.tile_pool(name="narrow", bufs=6))
         codes = ctx.enter_context(tc.tile_pool(name="codes", bufs=4))
-        slots = ctx.enter_context(tc.tile_pool(name="slots", bufs=3))
+        slots = ctx.enter_context(tc.tile_pool(name="slots", bufs=6))
+        prods = ctx.enter_context(tc.tile_pool(name="prods", bufs=2))
         sums = ctx.enter_context(tc.tile_pool(name="sums", bufs=1))
         psum = ctx.enter_context(tc.psum_pool(name="psum", bufs=8))
 
@@ -52,6 +52,8 @@ def tile_moe_tk_lin_bias_kernel(tc, xT, w, b, gate, offs, pos1, pos2, pos3, pos4
             return raw
 
         nc.gpsimd.memset(x_bytes[:], 0)
+        ident = keep.tile([P, P], F32, name="ident")
+        make_identity(nc, ident[:])
         x_raw = [load(xT[:, :N])]
         nc.sync.dma_start(offs_sb[:], offs)
         x_raw.append(load(xT[:, N:]))
@@ -71,7 +73,10 @@ def tile_moe_tk_lin_bias_kernel(tc, xT, w, b, gate, offs, pos1, pos2, pos3, pos4
 
         def group(copy, raw, start, width):
             grouped = (wide if width == 2 * P else narrow).tile([P, width, PACK], BF16, name="grouped", align_bytes=64)
-            copy(out=grouped[:], in_=raw[:, :, start : start + width].rearrange("p j c -> p c j"))
+            copy(
+                out=grouped[:].rearrange("p (c i) j -> p c j i", i=4),
+                in_=raw[:, :, start : start + width].rearrange("p j (c i) -> p c j i", i=4),
+            )
             return grouped
 
         def quantize(words, scales, grouped):
@@ -98,7 +103,7 @@ def tile_moe_tk_lin_bias_kernel(tc, xT, w, b, gate, offs, pos1, pos2, pos3, pos4
                 words = codes.tile([P, N], U32, name="words", align_bytes=64)
                 scales = codes.tile([P, N], U8, name="scales", align_bytes=64)
                 for start, width in PARTS:
-                    on_vector = width == P and e in VECTOR_NARROW
+                    on_vector = width == P and e % 3 == 2
                     grouped = group(nc.vector.tensor_copy if on_vector else nc.scalar.copy, w_raw[e], start, width)
                     quantize(words[:, start : start + width], scales[:, start : start + width], grouped)
                 for m in range(BANDS):
@@ -114,7 +119,7 @@ def tile_moe_tk_lin_bias_kernel(tc, xT, w, b, gate, offs, pos1, pos2, pos3, pos4
                     )
             experts = slice(team * TEAM, (team + 1) * TEAM)
             for m in range(BANDS):
-                if team in SCALAR_TEAMS:
+                if team == E // TEAM - 1 and m > 0:
                     for q in range(TEAM):
                         e = team * TEAM + q
                         nc.scalar.activation(
@@ -129,25 +134,50 @@ def tile_moe_tk_lin_bias_kernel(tc, xT, w, b, gate, offs, pos1, pos2, pos3, pos4
                     )
 
         H = T // 2
-        lo, hi = slice(0, H), slice(H, T)
+        lo, hi, whole = slice(0, H), slice(H, T), slice(0, T)
+
+        def fetch(prod, m, r, c):
+            o = pos_sb[r][:, c.start // 16 : c.stop // 16]
+            nc.vector.tensor_tensor(prod[r][:, c], y[m][:].indirect(o), gates[m * TOP + r][:, c], MULT)
+
         for m in range(BANDS):
-            prod = [sums.tile([P, T], F32, name=f"prod{r}") for r in range(TOP)]
-            first = sums.tile([P, T], F32, name="first")
-            second = sums.tile([P, T], F32, name="second")
+            prod = [prods.tile([P, T], F32, name=f"prod{r}") for r in range(TOP)]
             total = sums.tile([P, T], F32, name="total")
-
-            def fetch(r, c):
-                o = pos_sb[r][:, c.start // 16 : c.stop // 16]
-                nc.vector.tensor_tensor(prod[r][:, c], y[m][:].indirect(o), gates[m * TOP + r][:, c], MULT)
-
-            whole = slice(0, T)
-            fetch(0, whole)
-            fetch(1, whole)
-            fetch(2, whole)
-            nc.vector.tensor_add(first[:], prod[0][:], prod[1][:])
-            fetch(3, lo)
-            nc.vector.tensor_add(second[:], first[:], prod[2][:])
-            fetch(3, hi)
-            for c in (lo, hi):
-                nc.vector.tensor_add(total[:, c], second[:, c], prod[3][:, c])
-                nc.sync.dma_start(out[m * P : (m + 1) * P, c], total[:, c])
+            if m < 2:
+                turned = sums.tile([P, T], F32, name="turned")
+                for r in range(TOP):
+                    fetch(prod, m, r, whole)
+                for t0, n in ((0, 4), (4, 2)):
+                    cols = slice(t0 * P, (t0 + n) * P)
+                    acc = psum.tile([P, 4, P], F32, name="bank")
+                    for i in range(n):
+                        for r in range(TOP):
+                            nc.tensor.matmul(
+                                acc[:, i, :],
+                                lhsT=prod[r][:, (t0 + i) * P : (t0 + i + 1) * P],
+                                rhs=ident[:],
+                                start=r == 0,
+                                stop=r == TOP - 1,
+                                is_transpose=True,
+                            )
+                    nc.scalar.copy(turned[:, cols], acc[:, :n, :].rearrange("p i t -> p (i t)"))
+                for t0, n in ((0, 4), (4, 2)):
+                    cols = slice(t0 * P, (t0 + n) * P)
+                    back = psum.tile([P, 4, P], F32, name="bank")
+                    for i in range(n):
+                        nc.tensor.transpose(back[:, i, :], turned[:, (t0 + i) * P : (t0 + i + 1) * P], ident[:])
+                    nc.scalar.copy(total[:, cols], back[:, :n, :].rearrange("p i t -> p (i t)"))
+                nc.sync.dma_start(out[m * P : (m + 1) * P, :], total[:])
+            else:
+                first = sums.tile([P, T], F32, name="first")
+                second = sums.tile([P, T], F32, name="second")
+                fetch(prod, m, 0, whole)
+                fetch(prod, m, 1, whole)
+                fetch(prod, m, 2, whole)
+                nc.vector.tensor_add(first[:], prod[0][:], prod[1][:])
+                fetch(prod, m, 3, lo)
+                nc.vector.tensor_add(second[:], first[:], prod[2][:])
+                fetch(prod, m, 3, hi)
+                for c in (lo, hi):
+                    nc.vector.tensor_add(total[:, c], second[:, c], prod[3][:, c])
+                    nc.sync.dma_start(out[m * P : (m + 1) * P, c], total[:, c])

@@ -23,6 +23,8 @@ BANDS = N // P
 TEAM = 4
 GATHER = TEAM * C
 PARTS = ((0, 2 * P), (2 * P, P))
+BLOCKS = ((0, 4), (4, 2))
+LAST_PARTS = ((0, P), (P, P), (2 * P, P))
 
 
 def tile_moe_tk_lin_bias_kernel(tc, xT, w, b, gate, offs, pos1, pos2, pos3, pos4, out):
@@ -102,8 +104,8 @@ def tile_moe_tk_lin_bias_kernel(tc, xT, w, b, gate, offs, pos1, pos2, pos3, pos4
                 s = slice(q * C, (q + 1) * C)
                 words = codes.tile([P, N], U32, name="words", align_bytes=64)
                 scales = codes.tile([P, N], U8, name="scales", align_bytes=64)
-                for start, width in PARTS:
-                    on_vector = width == P and e % 3 == 2
+                for start, width in LAST_PARTS if e == E - 1 else PARTS:
+                    on_vector = start == 2 * P and e % 3 == 2
                     grouped = group(nc.vector.tensor_copy if on_vector else nc.scalar.copy, w_raw[e], start, width)
                     quantize(words[:, start : start + width], scales[:, start : start + width], grouped)
                 for m in range(BANDS):
@@ -140,44 +142,51 @@ def tile_moe_tk_lin_bias_kernel(tc, xT, w, b, gate, offs, pos1, pos2, pos3, pos4
             o = pos_sb[r][:, c.start // 16 : c.stop // 16]
             nc.vector.tensor_tensor(prod[r][:, c], y[m][:].indirect(o), gates[m * TOP + r][:, c], MULT)
 
+        def add_turned(acc, i, rows):
+            for n, prod in enumerate(rows):
+                nc.tensor.matmul(
+                    acc,
+                    lhsT=prod[:, i * P : (i + 1) * P],
+                    rhs=ident[:],
+                    start=n == 0,
+                    stop=n == len(rows) - 1,
+                    is_transpose=True,
+                )
+
+        def add_on_tensor(rows):
+            turned = sums.tile([P, T], F32, name="turned")
+            backs = []
+            for t0, n in BLOCKS:
+                acc = psum.tile([P, 4, P], F32, name="bank")
+                for i in range(n):
+                    add_turned(acc[:, i, :], t0 + i, rows)
+                nc.scalar.copy(turned[:, t0 * P : (t0 + n) * P], acc[:, :n, :].rearrange("p i t -> p (i t)"))
+            for t0, n in BLOCKS:
+                back = psum.tile([P, 4, P], F32, name="bank")
+                for i in range(n):
+                    nc.tensor.transpose(back[:, i, :], turned[:, (t0 + i) * P : (t0 + i + 1) * P], ident[:])
+                backs.append((slice(t0 * P, (t0 + n) * P), back[:, :n, :].rearrange("p i t -> p (i t)")))
+            return backs
+
         for m in range(BANDS):
             prod = [prods.tile([P, T], F32, name=f"prod{r}") for r in range(TOP)]
             total = sums.tile([P, T], F32, name="total")
-            if m < 2:
-                turned = sums.tile([P, T], F32, name="turned")
-                for r in range(TOP):
-                    fetch(prod, m, r, whole)
-                for t0, n in ((0, 4), (4, 2)):
-                    cols = slice(t0 * P, (t0 + n) * P)
-                    acc = psum.tile([P, 4, P], F32, name="bank")
-                    for i in range(n):
-                        for r in range(TOP):
-                            nc.tensor.matmul(
-                                acc[:, i, :],
-                                lhsT=prod[r][:, (t0 + i) * P : (t0 + i + 1) * P],
-                                rhs=ident[:],
-                                start=r == 0,
-                                stop=r == TOP - 1,
-                                is_transpose=True,
-                            )
-                    nc.scalar.copy(turned[:, cols], acc[:, :n, :].rearrange("p i t -> p (i t)"))
-                for t0, n in ((0, 4), (4, 2)):
-                    cols = slice(t0 * P, (t0 + n) * P)
-                    back = psum.tile([P, 4, P], F32, name="bank")
-                    for i in range(n):
-                        nc.tensor.transpose(back[:, i, :], turned[:, (t0 + i) * P : (t0 + i + 1) * P], ident[:])
-                    nc.scalar.copy(total[:, cols], back[:, :n, :].rearrange("p i t -> p (i t)"))
+            fetch(prod, m, 0, whole)
+            fetch(prod, m, 1, whole)
+            if m < BANDS - 1:
+                fetch(prod, m, 2, whole)
+                fetch(prod, m, 3, whole)
+                for cols, back in add_on_tensor(prod):
+                    nc.scalar.copy(total[:, cols], back)
                 nc.sync.dma_start(out[m * P : (m + 1) * P, :], total[:])
             else:
-                first = sums.tile([P, T], F32, name="first")
-                second = sums.tile([P, T], F32, name="second")
-                fetch(prod, m, 0, whole)
-                fetch(prod, m, 1, whole)
+                backs = add_on_tensor(prod[:2])
                 fetch(prod, m, 2, whole)
-                nc.vector.tensor_add(first[:], prod[0][:], prod[1][:])
                 fetch(prod, m, 3, lo)
-                nc.vector.tensor_add(second[:], first[:], prod[2][:])
+                three = sums.tile([P, T], F32, name="three")
+                for cols, back in backs:
+                    nc.vector.tensor_add(three[:, cols], back, prod[2][:, cols])
                 fetch(prod, m, 3, hi)
                 for c in (lo, hi):
-                    nc.vector.tensor_add(total[:, c], second[:, c], prod[3][:, c])
+                    nc.vector.tensor_add(total[:, c], three[:, c], prod[3][:, c])
                     nc.sync.dma_start(out[m * P : (m + 1) * P, c], total[:, c])

from contextlib import ExitStack

import concourse.mybir as mybir
from concourse.masks import make_identity

K, T, E, C, N = 512, 768, 24, 128, 384
TOP = 4
SLOTS = E * C
P = 128
PACK = 4
FLOPS = 2 * K * N * SLOTS

F32 = mybir.dt.float32
BF16 = mybir.dt.bfloat16
U32 = mybir.dt.uint32
U16 = mybir.dt.uint16
U8 = mybir.dt.uint8
FP8X4 = mybir.dt.float8_e4m3fn_x4
ADD, MULT = mybir.AluOpType.add, mybir.AluOpType.mult
IDENTITY = mybir.ActivationFunctionType.Identity

BANDS = N // P
TEAM = 4
GATHER = TEAM * C
PARTS = ((0, 2 * P), (2 * P, P))
BLOCKS = ((0, 4), (4, 2))
LAST_PARTS = ((0, P), (P, P), (2 * P, P))


def tile_moe_tk_lin_bias_kernel(tc, xT, w, b, gate, offs, pos1, pos2, pos3, pos4, out):
    nc = tc.nc
    with ExitStack() as ctx:
        lists = ctx.enter_context(tc.tile_pool(name="lists", bufs=1))
        keep = ctx.enter_context(tc.tile_pool(name="keep", bufs=1))
        stage = ctx.enter_context(tc.tile_pool(name="stage", bufs=18))
        wide = ctx.enter_context(tc.tile_pool(name="wide", bufs=8))
        narrow = ctx.enter_context(tc.tile_pool(name="narrow", bufs=6))
        codes = ctx.enter_context(tc.tile_pool(name="codes", bufs=4))
        slots = ctx.enter_context(tc.tile_pool(name="slots", bufs=6))
        prods = ctx.enter_context(tc.tile_pool(name="prods", bufs=2))
        sums = ctx.enter_context(tc.tile_pool(name="sums", bufs=1))
        psum = ctx.enter_context(tc.psum_pool(name="psum", bufs=8))

        offs_sb = lists.tile([P, SLOTS // 16], U16, name="offs_sb")
        pos_sb = [lists.tile([P, T // 16], U16, name=f"pos{r}_sb") for r in range(TOP)]
        bias = keep.tile([P, BANDS, E], F32, name="bias")
        x_words = keep.tile([P, T], U32, name="x_words", align_bytes=64)
        x_bytes = keep.tile([P, T], U8, name="x_bytes", align_bytes=64)
        y = [keep.tile([P, SLOTS], F32, name=f"y{m}") for m in range(BANDS)]

        def load(source):
            raw = stage.tile([P, PACK, N], F32, name="raw")
            nc.sync.dma_start(raw[:], source.rearrange("(p j) c -> p j c", j=PACK))
            return raw

        nc.gpsimd.memset(x_bytes[:], 0)
        ident = keep.tile([P, P], F32, name="ident")
        make_identity(nc, ident[:])
        x_raw = [load(xT[:, :N])]
        nc.sync.dma_start(offs_sb[:], offs)
        x_raw.append(load(xT[:, N:]))
        w_raw = [load(w[0])]
        nc.sync.dma_start(bias[:], b.rearrange("(m p) e -> p m e", p=P))
        for e in range(1, E):
            w_raw.append(load(w[e]))
        for pos_tile, pos in zip(pos_sb, (pos1, pos2, pos3, pos4)):
            nc.sync.dma_start(pos_tile[:], pos)
        gates = []
        for m in range(BANDS):
            for r in range(TOP):
                if r % 2 == 0:
                    pair = stage.tile([P, 2, T], F32, name="raw")
                nc.sync.dma_start(pair[:, r % 2, :], gate[r, m * P : (m + 1) * P, :])
                gates.append(pair[:, r % 2, :])

        def group(copy, raw, start, width):
            grouped = (wide if width == 2 * P else narrow).tile([P, width, PACK], BF16, name="grouped", align_bytes=64)
            copy(
                out=grouped[:].rearrange("p (c i) j -> p c j i", i=4),
                in_=raw[:, :, start : start + width].rearrange("p j (c i) -> p c j i", i=4),
            )
            return grouped

        def quantize(words, scales, grouped):
            nc.vector.quantize_mx(
                out=words.bitcast(FP8X4), scales=scales, in_=grouped[:].rearrange("p c j -> p (c j)")
            )

        for h in range(2):
            for start, width in PARTS:
                tokens = slice(h * N + start, h * N + start + width)
                grouped = group(nc.vector.tensor_copy, x_raw[h], start, width)
                quantize(x_words[:, tokens], x_bytes[:, tokens], grouped)

        for team in range(E // TEAM):
            o = offs_sb[:, team * GATHER // 16 : (team + 1) * GATHER // 16]
            slot_words = slots.tile([P, GATHER], U32, name="slot_words", align_bytes=64)
            nc.vector.tensor_copy(slot_words[:], x_words[:].indirect(o))
            slot_bytes = slots.tile([P, GATHER], U8, name="slot_bytes", align_bytes=64)
            nc.vector.tensor_copy(slot_bytes[:], x_bytes[:].indirect(o))
            banks = [psum.tile([P, TEAM, C], F32, name="bank") for m in range(BANDS)]
            for q in range(TEAM):
                e = team * TEAM + q
                s = slice(q * C, (q + 1) * C)
                words = codes.tile([P, N], U32, name="words", align_bytes=64)
                scales = codes.tile([P, N], U8, name="scales", align_bytes=64)
                for start, width in LAST_PARTS if e == E - 1 else PARTS:
                    on_vector = start == 2 * P and e % 3 == 2
                    grouped = group(nc.vector.tensor_copy if on_vector else nc.scalar.copy, w_raw[e], start, width)
                    quantize(words[:, start : start + width], scales[:, start : start + width], grouped)
                for m in range(BANDS):
                    rows = slice(m * P, (m + 1) * P)
                    nc.tensor.matmul_mx(
                        out=banks[m][:, q, :],
                        lhsT=words[:, rows].bitcast(FP8X4),
                        lhsT_scale=scales[:, rows],
                        rhs=slot_words[:, s].bitcast(FP8X4),
                        rhs_scale=slot_bytes[:, s],
                        start=True,
                        stop=True,
                    )
            experts = slice(team * TEAM, (team + 1) * TEAM)
            for m in range(BANDS):
                if team == E // TEAM - 1 and m > 0:
                    for q in range(TEAM):
                        e = team * TEAM + q
                        nc.scalar.activation(
                            y[m][:, e * C : (e + 1) * C], banks[m][:, q, :], IDENTITY, bias=bias[:, m, e : e + 1]
                        )
                else:
                    nc.vector.tensor_tensor(
                        y[m][:, team * GATHER : (team + 1) * GATHER].rearrange("p (q c) -> p q c", q=TEAM),
                        banks[m][:],
                        bias[:, m, experts].unsqueeze(2).to_broadcast([P, TEAM, C]),
                        ADD,
                    )

        H = T // 2
        lo, hi, whole = slice(0, H), slice(H, T), slice(0, T)

        def fetch(prod, m, r, c):
            o = pos_sb[r][:, c.start // 16 : c.stop // 16]
            nc.vector.tensor_tensor(prod[r][:, c], y[m][:].indirect(o), gates[m * TOP + r][:, c], MULT)

        def add_turned(acc, i, rows):
            for n, prod in enumerate(rows):
                nc.tensor.matmul(
                    acc,
                    lhsT=prod[:, i * P : (i + 1) * P],
                    rhs=ident[:],
                    start=n == 0,
                    stop=n == len(rows) - 1,
                    is_transpose=True,
                )

        def add_on_tensor(rows):
            turned = sums.tile([P, T], F32, name="turned")
            backs = []
            for t0, n in BLOCKS:
                acc = psum.tile([P, 4, P], F32, name="bank")
                for i in range(n):
                    add_turned(acc[:, i, :], t0 + i, rows)
                nc.scalar.copy(turned[:, t0 * P : (t0 + n) * P], acc[:, :n, :].rearrange("p i t -> p (i t)"))
            for t0, n in BLOCKS:
                back = psum.tile([P, 4, P], F32, name="bank")
                for i in range(n):
                    nc.tensor.transpose(back[:, i, :], turned[:, (t0 + i) * P : (t0 + i + 1) * P], ident[:])
                backs.append((slice(t0 * P, (t0 + n) * P), back[:, :n, :].rearrange("p i t -> p (i t)")))
            return backs

        for m in range(BANDS):
            prod = [prods.tile([P, T], F32, name=f"prod{r}") for r in range(TOP)]
            total = sums.tile([P, T], F32, name="total")
            fetch(prod, m, 0, whole)
            fetch(prod, m, 1, whole)
            if m < BANDS - 1:
                fetch(prod, m, 2, whole)
                fetch(prod, m, 3, whole)
                for cols, back in add_on_tensor(prod):
                    nc.scalar.copy(total[:, cols], back)
                nc.sync.dma_start(out[m * P : (m + 1) * P, :], total[:])
            else:
                backs = add_on_tensor(prod[:2])
                fetch(prod, m, 2, whole)
                fetch(prod, m, 3, lo)
                three = sums.tile([P, T], F32, name="three")
                for cols, back in backs:
                    nc.vector.tensor_add(three[:, cols], back, prod[2][:, cols])
                fetch(prod, m, 3, hi)
                for c in (lo, hi):
                    nc.vector.tensor_add(total[:, c], three[:, c], prod[3][:, c])
                    nc.sync.dma_start(out[m * P : (m + 1) * P, c], total[:, c])
